import numpy as np
import ml_dtypes


def mxq(x, axis, fmt="e4m3"):
    dtype, down = {"e4m3": (ml_dtypes.float8_e4m3fn, 7), "e5m2": (ml_dtypes.float8_e5m2, 14)}[fmt]
    v = np.moveaxis(np.asarray(x, np.float32).astype(ml_dtypes.bfloat16).astype(np.float64), axis, -1)
    blocks = v.reshape(v.shape[:-1] + (-1, 32))
    amax = np.abs(blocks).max(-1, keepdims=True)
    byte = np.maximum(np.where(amax > 0, np.frexp(amax)[1] - 1 + 127, 0) - down, 1)
    scale = np.exp2(byte - 127.0)
    codes = (blocks / scale).astype(np.float32).astype(dtype).astype(np.float64)
    return np.moveaxis((codes * scale).reshape(v.shape), -1, axis)


WIDE = False


def mx_kscale(k):
    if not WIDE:
        return np.ones(k)
    levels = np.array([10, -10, 5, -5, 0])
    if k % 512:
        return np.exp2(np.random.permutation(np.resize(levels, k // 32))).repeat(32)
    a = np.empty((k // 512, 16))
    for p in range(k // 512):
        a[p, :8] = np.random.permutation(np.resize(levels, 8))
        for g in range(8):
            far = levels[np.abs(levels - a[p, g]) >= 10]
            a[p, g + 8] = far[np.random.randint(len(far))]
    return np.exp2(a.ravel()).repeat(32)


def f64(x):
    return np.asarray(x).astype(np.float64)


def striped(idx):
    return np.tile(idx.reshape(-1, 16).T, (8, 1)).astype(np.uint16)


def unstriped(offs):
    return offs[:16].T.reshape(-1).astype(np.int64)


def striped8(idx):
    return np.concatenate([x.reshape(-1, 16).T for x in idx]).astype(np.uint16)


def runs(offs, k):
    lists = np.stack([offs[16 * r : 16 * r + 16].T.reshape(-1) for r in range(8)]).astype(np.int64)
    return lists[np.arange(k) % 512 // 64]


def pack_weight(w):
    k, n = w.shape
    w = f64(np.asarray(w, np.float32).astype(ml_dtypes.bfloat16)).reshape(k // 32, 32, n)
    amax = np.abs(w).max(1)
    byte = np.clip(np.where(amax > 0, np.frexp(amax)[1] - 1 + 127 - 7, 1), 1, 254)
    scaled = (w * np.exp2(127.0 - byte)[:, None, :]).reshape(k, n).astype(np.float32)
    words = np.ascontiguousarray(scaled.reshape(k // 512, 128, 4, n).transpose(0, 1, 3, 2)).astype(ml_dtypes.float8_e4m3fn).view(np.uint8)
    return words, np.ascontiguousarray(byte.astype(np.uint8).reshape(k // 512, 16, n))


def unpack_weight(words, scales):
    g, p, n, _ = words.shape
    vals = np.ascontiguousarray(words).view(ml_dtypes.float8_e4m3fn).astype(np.float64) * np.repeat(np.exp2(scales.astype(np.float64) - 127.0), 8, axis=1)[..., None]
    return vals.transpose(0, 1, 3, 2).reshape(g * 512, n)


K, T, S, V, H = 512, 2048, 512, 512, 512


def setup_inputs():
    n = np.random.standard_normal
    s = mx_kscale(K)[:, None]
    u = mx_kscale(S)
    packed_xT = pack_weight(n((K, T)) * s)
    return {
        "x_words": packed_xT[0],
        "x_scales": packed_xT[1],
        "w1": (n((K, H)) / np.sqrt(K) / s).astype(np.float32),
        "w2": (n((K, H)) / np.sqrt(K) / s).astype(np.float32),
        "w3": (n((K, H)) / np.sqrt(K) / s).astype(np.float32),
        "ga": (np.random.uniform(0.5, 1.5, (H, 1)) * u[:, None]).astype(np.float32),
        "gb": (np.random.uniform(0.5, 1.5, (H, 1)) / u[:, None]).astype(np.float32),
        "offs": striped(np.random.permutation(T)[:S]),
        "two": striped(np.random.permutation(T)[:S]),
        "n1": striped8(np.stack([np.random.permutation(S) for _ in range(8)])),
        "n2": striped8(np.stack([np.random.permutation(S) for _ in range(8)])),
        "three": striped(np.random.permutation(T)[:V]),
        "n3": striped8(np.stack([np.random.permutation(V) for _ in range(8)])),
        "n4": striped8(np.stack([np.random.permutation(V) for _ in range(8)])),
        "n5": striped8(np.stack([np.random.permutation(V) for _ in range(8)])),
        "n6": striped8(np.stack([np.random.permutation(V) for _ in range(8)])),
    }


def reference(x_words, x_scales, w1, w2, w3, ga, gb, offs, two, n1, n2, three, n3, n4, n5, n6):
    xq = unpack_weight(x_words, x_scales)[:, unstriped(offs)]
    y = mxq(f64(w1), 0, "e4m3").T @ xq
    x_two = unpack_weight(x_words, x_scales)[:, unstriped(two)]
    d = mxq(f64(w2), 0, "e4m3").T @ x_two
    z = f64(ga) * (0.75 * (y * (d[np.arange(H)[:, None], runs(n2, H)]) - ((y[np.arange(H)[:, None], runs(n1, H)]) * d)))
    x_three = unpack_weight(x_words, x_scales)[:, unstriped(three)]
    b = mxq(f64(w3), 0, "e4m3").T @ x_three
    st = b - (b[np.arange(H)[:, None], runs(n3, H)])
    z2 = f64(gb) * (st / (np.abs(st[np.arange(H)[:, None], runs(n4, H)]) + 0.5))
    s = 0.0625 * ((mxq(z, 0, "e4m3").T @ mxq(z2, 0, "e4m3")))
    st2 = np.maximum(s, s[np.arange(S)[:, None], runs(n5, S)])
    return st2[np.arange(S)[:, None], runs(n6, S)] - (0.5 * s)

@@ -1,0 +1,224 @@
+from contextlib import ExitStack
+
+import concourse.mybir as mybir
+
+F32 = mybir.dt.float32
+BF16 = mybir.dt.bfloat16
+I32 = mybir.dt.int32
+U32 = mybir.dt.uint32
+U16 = mybir.dt.uint16
+U8 = mybir.dt.uint8
+FP8X4 = mybir.dt.float8_e4m3fn_x4
+ALU = mybir.AluOpType
+ACT = mybir.ActivationFunctionType
+
+P = 128
+PACK = 4
+T = 2048
+W = 512
+HALF = W // 2
+LCOLS = HALF // 16
+
+FLOPS = 4 * 2 * 512 * 512 * 512
+
+
+def tile_picked_twkcrossbhopnhopb_none_p_kernel(tc, x_words, x_scales, w1, w2, w3, ga, gb, offs, two, n1, n2, three, n3, n4, n5, n6, out):
+    nc = tc.nc
+    with ExitStack() as ctx:
+        keep = ctx.enter_context(tc.tile_pool(name="keep", bufs=1))
+        psum = ctx.enter_context(tc.psum_pool(name="psum", bufs=8))
+
+        def load_list(src, name):
+            tile = keep.tile([P, W // 16], U16, name=name)
+            nc.sync.dma_start(tile[:], src)
+            return tile
+
+        def load_weight(src, name):
+            tile = keep.tile([P, PACK, W], F32, name=name)
+            nc.sync.dma_start(tile[:], src.rearrange("(p j) c -> p j c", j=PACK))
+            return tile
+
+        def load_rows(src, name):
+            tile = keep.tile([P, PACK], F32, name=name)
+            nc.sync.dma_start(tile[:], src.rearrange("(p t) o -> p (t o)", t=PACK))
+            return tile
+
+        xs = keep.tile([P, T], U8, name="xs")
+        nc.vector.memset(xs[:, : T // 2].bitcast(I32), 0)
+        nc.gpsimd.memset(xs[:, T // 2 :].bitcast(I32), 0)
+        l_three = load_list(three, "l_three")
+        l_offs = load_list(offs, "l_offs")
+        l_two = load_list(two, "l_two")
+        gb_t = load_rows(gb, "gb_t")
+        xw = keep.tile([P, T], I32, name="xw")
+        nc.sync.dma_start(xw[:], x_words[0].rearrange("p n t -> p (n t)").bitcast(I32))
+        for q in range(4):
+            nc.scalar.dma_start(xs[32 * q : 32 * q + 4, :].bitcast(I32), x_scales[0, 4 * q : 4 * q + 4, :].bitcast(I32))
+        w3_raw = load_weight(w3, "w3_raw")
+        w1_raw = load_weight(w1, "w1_raw")
+        l_n3 = load_list(n3, "l_n3")
+        w2_raw = load_weight(w2, "w2_raw")
+        ga_t = load_rows(ga, "ga_t")
+        l_n1 = load_list(n1, "l_n1")
+        l_n2 = load_list(n2, "l_n2")
+        l_n4 = load_list(n4, "l_n4")
+        l_n5 = load_list(n5, "l_n5")
+        l_n6 = load_list(n6, "l_n6")
+
+        def pick_words(lst, name):
+            words = keep.tile([P, W], U32, name=name + "_w", align_bytes=64)
+            nc.vector.tensor_copy(words[:], xw[:].bitcast(U32).indirect(lst[:]))
+            return words
+
+        def pick_scales(lst, name):
+            scales = keep.tile([P, W], U8, name=name + "_s", align_bytes=64)
+            nc.vector.tensor_copy(scales[:], xs[:].indirect(lst[:]))
+            return scales
+
+        def weave(raw, name, on_scalar):
+            grouped = keep.tile([P, PACK * W], BF16, name=name, align_bytes=64)
+            dst = grouped[:].rearrange("p (t m j) -> p m j t", t=PACK, j=PACK)
+            src = raw[:].rearrange("p j (m t) -> p m j t", t=PACK)
+            if on_scalar:
+                nc.scalar.copy(dst, src)
+            else:
+                nc.vector.tensor_copy(dst, src)
+            return grouped
+
+        def quantize(grouped, width, name):
+            codes = keep.tile([P, width], U32, name=name + "_c", align_bytes=64)
+            scales = keep.tile([P, width], U8, name=name + "_s", align_bytes=64)
+            nc.vector.quantize_mx(out=codes[:].bitcast(FP8X4), scales=scales[:], in_=grouped[:])
+            return codes, scales
+
+        def product(lhs, col, rhs):
+            acc = psum.tile([P, W], F32, name="acc")
+            nc.tensor.matmul_mx(
+                out=acc[:],
+                lhsT=lhs[0][:, col : col + P].bitcast(FP8X4),
+                lhsT_scale=lhs[1][:, col : col + P],
+                rhs=rhs[0][:].bitcast(FP8X4),
+                rhs_scale=rhs[1][:],
+                start=True,
+                stop=True,
+            )
+            return acc
+
+        def half(lst, h):
+            return lst[:, h * LCOLS : (h + 1) * LCOLS]
+
+        def cols(h):
+            return slice(h * HALF, (h + 1) * HALF)
+
+        x3_w = pick_words(l_three, "x3")
+        x3 = (x3_w, pick_scales(l_three, "x3"))
+        w3_g = weave(w3_raw, "w3_g", True)
+        x1_w = pick_words(l_offs, "x1")
+        x2_w = pick_words(l_two, "x2")
+        w3_q = quantize(w3_g, W, "w3_q")
+        x1 = (x1_w, pick_scales(l_offs, "x1"))
+        x2 = (x2_w, pick_scales(l_two, "x2"))
+
+        ga75 = keep.tile([P, PACK], F32, name="ga75")
+        nc.vector.tensor_scalar(ga75[:], ga_t[:], 0.75, None, ALU.mult)
+        gb_safe = keep.tile([P, PACK], F32, name="gb_safe")
+        nc.vector.scalar_tensor_tensor(gb_safe[:], gb_t[:], 0.0, gb_t[:], ALU.is_equal, ALU.add)
+        gb_inv = keep.tile([P, PACK], F32, name="gb_inv")
+        nc.vector.reciprocal(gb_inv[:], gb_safe[:])
+
+        bg = []
+        for t in range(PACK):
+            acc = product(w3_q, t * P, x3)
+            tile = keep.tile([P, W], F32, name="bg%d" % t)
+            nc.scalar.activation(tile[:], acc[:], ACT.Copy, scale=gb_t[:, t : t + 1])
+            bg.append(tile)
+
+        g3 = keep.tile([P, PACK, W], F32, name="g3")
+        for t in range(PACK):
+            for h in range(2):
+                nc.scalar.activation(g3[:, t, cols(h)], bg[t][:].indirect(half(l_n3, h)), ACT.Copy)
+
+        w1_g = weave(w1_raw, "w1_g", False)
+        w2_g = weave(w2_raw, "w2_g", False)
+        w1_q = quantize(w1_g, W, "w1_q")
+        w2_q = quantize(w2_g, W, "w2_q")
+
+        stg = keep.tile([P, PACK, W], F32, name="stg")
+        za = keep.tile([P, PACK, W], F32, name="za")
+        zb = keep.tile([P, PACK, W], F32, name="zb")
+        size = keep.tile([P, PACK, W], F32, name="size")
+        ya, d = [], []
+        for t in range(PACK):
+            acc = product(w2_q, t * P, x2)
+            tile = keep.tile([P, W], F32, name="d%d" % t)
+            nc.scalar.copy(tile[:], acc[:])
+            d.append(tile)
+            acc = product(w1_q, t * P, x1)
+            tile = keep.tile([P, W], F32, name="ya%d" % t)
+            nc.vector.tensor_scalar(tile[:], acc[:], ga75[:, t : t + 1], None, ALU.mult)
+            ya.append(tile)
+            nc.vector.tensor_tensor(stg[:, t, :], bg[t][:], g3[:, t, :], ALU.subtract)
+        for t in range(PACK):
+            nc.scalar.activation(size[:, t, :], stg[:, t, :], ACT.Abs, scale=gb_inv[:, t : t + 1])
+        logs = []
+        for t in range(PACK):
+            tile = keep.tile([P, W], F32, name="log%d" % t)
+            nc.scalar.activation(tile[:], size[:, t, :], ACT.Ln, bias=0.5)
+            logs.append(tile)
+        inv = keep.tile([P, PACK, W], F32, name="inv")
+        for h in range(2):
+            for t in range(PACK):
+                nc.scalar.activation(inv[:, t, cols(h)], logs[t][:].indirect(half(l_n4, h)), ACT.Exp, scale=-1.0)
+
+        for t in range(PACK):
+            for h in range(2):
+                nc.vector.tensor_tensor(za[:, t, cols(h)], d[t][:].indirect(half(l_n2, h)), ya[t][:, cols(h)], ALU.mult)
+                nc.vector.tensor_tensor(zb[:, t, cols(h)], ya[t][:].indirect(half(l_n1, h)), d[t][:, cols(h)], ALU.mult)
+
+        def z_pair(h):
+            z_g = keep.tile([P, PACK * HALF], BF16, name="z_g%d" % h, align_bytes=64)
+            nc.vector.tensor_tensor(
+                z_g[:].rearrange("p (e m t) -> p m t e", e=2, t=PACK),
+                za[:].rearrange("p t (m h e) -> p h m t e", h=2, e=2)[:, h],
+                zb[:].rearrange("p t (m h e) -> p h m t e", h=2, e=2)[:, h],
+                ALU.subtract,
+            )
+            return z_g
+
+        z2_c = keep.tile([P, W], U32, name="z2_c", align_bytes=64)
+        z2_s = keep.tile([P, W], U8, name="z2_s", align_bytes=64)
+
+        def z2_half(h):
+            part = keep.tile([P, PACK * HALF], BF16, name="z2_g%d" % h, align_bytes=64)
+            nc.vector.tensor_tensor(
+                part[:].rearrange("p (c i t) -> p c t i", i=2, t=PACK),
+                stg[:, :, cols(h)].rearrange("p t (c i) -> p c t i", i=2),
+                inv[:, :, cols(h)].rearrange("p t (c i) -> p c t i", i=2),
+                ALU.mult,
+            )
+            return part
+
+        def z2_quantize(part, h):
+            nc.vector.quantize_mx(out=z2_c[:, cols(h)].bitcast(FP8X4), scales=z2_s[:, cols(h)], in_=part[:])
+
+        z_g0 = z_pair(0)
+        z2_g0 = z2_half(0)
+        z_q = [quantize(z_g0, HALF, "z_q0")]
+        z2_quantize(z2_g0, 0)
+        z2_quantize(z2_half(1), 1)
+        z_q.append(quantize(z_pair(1), HALF, "z_q1"))
+
+        out_rows = out.rearrange("(p t) v -> p t v", t=PACK)
+        for t in range(PACK):
+            acc = product(z_q[t // 2], (t % 2) * P, (z2_c, z2_s))
+            hs = keep.tile([P, W], F32, name="hs%d" % t)
+            nc.scalar.activation(hs[:], acc[:], ACT.Copy, scale=0.03125)
+            g5 = keep.tile([P, W], F32, name="g5%d" % t)
+            for h in range(2):
+                nc.scalar.activation(g5[:, cols(h)], hs[:].indirect(half(l_n5, h)), ACT.Copy, scale=2.0)
+            st2 = keep.tile([P, W], F32, name="st2%d" % t)
+            nc.vector.scalar_tensor_tensor(st2[:], hs[:], 2.0, g5[:], ALU.mult, ALU.max)
+            res = keep.tile([P, W], F32, name="res%d" % t)
+            for h in range(2):
+                nc.vector.tensor_tensor(res[:, cols(h)], st2[:].indirect(half(l_n6, h)), hs[:, cols(h)], ALU.subtract)
+            nc.sync.dma_start(out_rows[:, t, :], res[:])

@@ -17,7 +17,6 @@ PACK = 4
 T = 2048
 W = 512
 HALF = W // 2
-LCOLS = HALF // 16
 
 FLOPS = 4 * 2 * 512 * 512 * 512
 
@@ -26,37 +25,42 @@ def tile_picked_twkcrossbhopnhopb_none_p_kernel(tc, x_words, x_scales, w1, w2, w
     nc = tc.nc
     with ExitStack() as ctx:
         keep = ctx.enter_context(tc.tile_pool(name="keep", bufs=1))
-        psum = ctx.enter_context(tc.psum_pool(name="psum", bufs=8))
+        work = ctx.enter_context(tc.tile_pool(name="work", bufs=1))
+        psum = ctx.enter_context(tc.psum_pool(name="psum", bufs=1))
+
+        def tile(shape, dtype, name, tag=None):
+            return work.tile(shape, dtype, name=name, tag=tag or name, align_bytes=64)
 
         def load_list(src, name):
-            tile = keep.tile([P, W // 16], U16, name=name)
-            nc.sync.dma_start(tile[:], src)
-            return tile
+            lst = keep.tile([P, W // 16], U16, name=name)
+            nc.sync.dma_start(lst[:], src)
+            return lst
 
         def load_weight(src, name):
-            tile = keep.tile([P, PACK, W], F32, name=name)
-            nc.sync.dma_start(tile[:], src.rearrange("(p j) c -> p j c", j=PACK))
-            return tile
+            raw = tile([P, PACK, W], F32, name)
+            nc.sync.dma_start(raw[:], src.rearrange("(p j) c -> p j c", j=PACK))
+            return raw
 
         def load_rows(src, name):
-            tile = keep.tile([P, PACK], F32, name=name)
-            nc.sync.dma_start(tile[:], src.rearrange("(p t) o -> p (t o)", t=PACK))
-            return tile
+            rows = tile([P, 7], F32, name)
+            for e in range(2):
+                nc.sync.dma_start(rows[e:P:2, :], src.rearrange("(a c) o -> a (c o)", c=8)[:, e : e + 7])
+            return rows[:, 0:7:2]
 
-        xs = keep.tile([P, T], U8, name="xs")
+        xs = tile([P, T], U8, "xs")
         nc.vector.memset(xs[:, : T // 2].bitcast(I32), 0)
         nc.gpsimd.memset(xs[:, T // 2 :].bitcast(I32), 0)
         l_three = load_list(three, "l_three")
         l_offs = load_list(offs, "l_offs")
         l_two = load_list(two, "l_two")
-        gb_t = load_rows(gb, "gb_t")
-        xw = keep.tile([P, T], I32, name="xw")
+        l_n3 = load_list(n3, "l_n3")
+        xw = tile([P, T], I32, "xw")
         nc.sync.dma_start(xw[:], x_words[0].rearrange("p n t -> p (n t)").bitcast(I32))
         for q in range(4):
             nc.scalar.dma_start(xs[32 * q : 32 * q + 4, :].bitcast(I32), x_scales[0, 4 * q : 4 * q + 4, :].bitcast(I32))
         w3_raw = load_weight(w3, "w3_raw")
         w1_raw = load_weight(w1, "w1_raw")
-        l_n3 = load_list(n3, "l_n3")
+        gb_t = load_rows(gb, "gb_t")
         w2_raw = load_weight(w2, "w2_raw")
         ga_t = load_rows(ga, "ga_t")
         l_n1 = load_list(n1, "l_n1")
@@ -66,159 +70,177 @@ def tile_picked_twkcrossbhopnhopb_none_p_kernel(tc, x_words, x_scales, w1, w2, w
         l_n6 = load_list(n6, "l_n6")
 
         def pick_words(lst, name):
-            words = keep.tile([P, W], U32, name=name + "_w", align_bytes=64)
+            words = tile([P, W], U32, name)
             nc.vector.tensor_copy(words[:], xw[:].bitcast(U32).indirect(lst[:]))
-            return words
+            return words[:]
 
-        def pick_scales(lst, name):
-            scales = keep.tile([P, W], U8, name=name + "_s", align_bytes=64)
-            nc.vector.tensor_copy(scales[:], xs[:].indirect(lst[:]))
-            return scales
-
-        def weave(raw, name, on_scalar):
-            grouped = keep.tile([P, PACK * W], BF16, name=name, align_bytes=64)
-            dst = grouped[:].rearrange("p (t m j) -> p m j t", t=PACK, j=PACK)
-            src = raw[:].rearrange("p j (m t) -> p m j t", t=PACK)
-            if on_scalar:
-                nc.scalar.copy(dst, src)
-            else:
-                nc.vector.tensor_copy(dst, src)
-            return grouped
+        def pick_scales(lst, dst):
+            nc.vector.tensor_copy(dst, xs[:].indirect(lst[:]))
+            return dst
 
         def quantize(grouped, width, name):
-            codes = keep.tile([P, width], U32, name=name + "_c", align_bytes=64)
-            scales = keep.tile([P, width], U8, name=name + "_s", align_bytes=64)
-            nc.vector.quantize_mx(out=codes[:].bitcast(FP8X4), scales=scales[:], in_=grouped[:])
+            codes = tile([P, width], U32, name + "_c")
+            scales = tile([P, width], U8, name + "_s")
+            nc.vector.quantize_mx(out=codes[:].bitcast(FP8X4), scales=scales[:], in_=grouped)
             return codes, scales
 
-        def product(lhs, col, rhs):
-            acc = psum.tile([P, W], F32, name="acc")
+        def product(lhs, col, rhs, bank):
+            acc = psum.tile([P, W], F32, name="acc", tag="bank%d" % bank)
             nc.tensor.matmul_mx(
                 out=acc[:],
                 lhsT=lhs[0][:, col : col + P].bitcast(FP8X4),
                 lhsT_scale=lhs[1][:, col : col + P],
-                rhs=rhs[0][:].bitcast(FP8X4),
-                rhs_scale=rhs[1][:],
+                rhs=rhs[0].bitcast(FP8X4),
+                rhs_scale=rhs[1],
                 start=True,
                 stop=True,
             )
             return acc
 
-        def half(lst, h):
-            return lst[:, h * LCOLS : (h + 1) * LCOLS]
+        def entries(lst, a, b):
+            return lst[:, a // 16 : b // 16]
 
-        def cols(h):
-            return slice(h * HALF, (h + 1) * HALF)
+        halves = [(0, HALF), (HALF, W)]
 
-        x3_w = pick_words(l_three, "x3")
-        x3 = (x3_w, pick_scales(l_three, "x3"))
-        w3_g = weave(w3_raw, "w3_g", True)
-        x1_w = pick_words(l_offs, "x1")
-        x2_w = pick_words(l_two, "x2")
-        w3_q = quantize(w3_g, W, "w3_q")
-        x1 = (x1_w, pick_scales(l_offs, "x1"))
-        x2 = (x2_w, pick_scales(l_two, "x2"))
+        def weave(raw, name):
+            grouped = tile([P, PACK * W], BF16, name, "grouped")
+            nc.vector.tensor_copy(
+                grouped[:].rearrange("p (t a e j) -> p a t j e", t=PACK, e=2, j=PACK),
+                raw[:].rearrange("p j (a t e) -> p a t j e", t=PACK, e=2),
+            )
+            return grouped
 
-        ga75 = keep.tile([P, PACK], F32, name="ga75")
-        nc.vector.tensor_scalar(ga75[:], ga_t[:], 0.75, None, ALU.mult)
-        gb_safe = keep.tile([P, PACK], F32, name="gb_safe")
-        nc.vector.scalar_tensor_tensor(gb_safe[:], gb_t[:], 0.0, gb_t[:], ALU.is_equal, ALU.add)
-        gb_inv = keep.tile([P, PACK], F32, name="gb_inv")
+        x3_w = pick_words(l_three, "x3_w")
+        x3_s = tile([P, W], U8, "x3_s")
+        x3 = (x3_w, pick_scales(l_three, x3_s[:]))
+        w3_g = []
+        for h in range(2):
+            grouped = tile([P, PACK * HALF], BF16, "w3_g%d" % h, "grouped" if h else None)
+            for u in range(2):
+                nc.scalar.activation(
+                    grouped[:].rearrange("p (u a e j) -> p u a j e", u=2, e=2, j=PACK)[:, u],
+                    w3_raw[:].rearrange("p j (a t e) -> p t a j e", t=PACK, e=2)[:, 2 * h + u],
+                    ACT.Copy,
+                )
+            w3_g.append(grouped)
+        x1_w = pick_words(l_offs, "x1_w")
+        x2_w = pick_words(l_two, "x2_w")
+        w3_q = [quantize(w3_g[h][:], HALF, "w3_q%d" % h) for h in range(2)]
+        x12_s = tile([P, 2 * W], U8, "x12_s", "w3_raw")
+        x1 = (x1_w, pick_scales(l_offs, x12_s[:, :W]))
+
+        ga75 = tile([P, PACK], F32, "ga75")
+        nc.vector.tensor_scalar(ga75[:], ga_t, 0.75, None, ALU.mult)
+        gb_safe = tile([P, PACK], F32, "gb_safe")
+        nc.vector.scalar_tensor_tensor(gb_safe[:], gb_t, 0.0, gb_t, ALU.is_equal, ALU.add)
+        gb_inv = tile([P, PACK], F32, "gb_inv")
         nc.vector.reciprocal(gb_inv[:], gb_safe[:])
 
         bg = []
         for t in range(PACK):
-            acc = product(w3_q, t * P, x3)
-            tile = keep.tile([P, W], F32, name="bg%d" % t)
-            nc.scalar.activation(tile[:], acc[:], ACT.Copy, scale=gb_t[:, t : t + 1])
-            bg.append(tile)
+            acc = product(w3_q[t // 2], (t % 2) * P, x3, t)
+            rows = tile([P, W], F32, "bg%d" % t)
+            nc.scalar.activation(rows[:], acc[:], ACT.Copy, scale=gb_t[:, t : t + 1])
+            bg.append(rows)
 
-        g3 = keep.tile([P, PACK, W], F32, name="g3")
+        w1_g = weave(w1_raw, "w1_g")
+        x2 = (x2_w, pick_scales(l_two, x12_s[:, W:]))
+        w1_q = quantize(w1_g[:], W, "w1_q")
+        w2_q = quantize(weave(w2_raw, "w2_g")[:], W, "w2_q")
+
+        g3 = []
         for t in range(PACK):
-            for h in range(2):
-                nc.scalar.activation(g3[:, t, cols(h)], bg[t][:].indirect(half(l_n3, h)), ACT.Copy)
+            rows = tile([P, W], F32, "g3%d" % t)
+            for a, b in halves:
+                nc.scalar.activation(rows[:, a:b], bg[t][:].indirect(entries(l_n3, a, b)), ACT.Copy)
+            g3.append(rows)
 
-        w1_g = weave(w1_raw, "w1_g", False)
-        w2_g = weave(w2_raw, "w2_g", False)
-        w1_q = quantize(w1_g, W, "w1_q")
-        w2_q = quantize(w2_g, W, "w2_q")
-
-        stg = keep.tile([P, PACK, W], F32, name="stg")
-        za = keep.tile([P, PACK, W], F32, name="za")
-        zb = keep.tile([P, PACK, W], F32, name="zb")
-        size = keep.tile([P, PACK, W], F32, name="size")
         ya, d = [], []
         for t in range(PACK):
-            acc = product(w2_q, t * P, x2)
-            tile = keep.tile([P, W], F32, name="d%d" % t)
-            nc.scalar.copy(tile[:], acc[:])
-            d.append(tile)
-            acc = product(w1_q, t * P, x1)
-            tile = keep.tile([P, W], F32, name="ya%d" % t)
-            nc.vector.tensor_scalar(tile[:], acc[:], ga75[:, t : t + 1], None, ALU.mult)
-            ya.append(tile)
-            nc.vector.tensor_tensor(stg[:, t, :], bg[t][:], g3[:, t, :], ALU.subtract)
+            acc = product(w1_q, t * P, x1, 4 + t)
+            rows = tile([P, W], F32, "ya%d" % t)
+            if t < 2:
+                nc.vector.tensor_scalar(rows[:], acc[:], ga75[:, t : t + 1], None, ALU.mult)
+            else:
+                nc.scalar.activation(rows[:], acc[:], ACT.Copy, scale=ga75[:, t : t + 1])
+            ya.append(rows)
+            acc = product(w2_q, t * P, x2, (6 + t) % 8)
+            rows = tile([P, W], F32, "d%d" % t)
+            nc.scalar.copy(rows[:], acc[:])
+            d.append(rows)
+
+        stg = tile([P, PACK, W], F32, "stg")
+        for t in range(PACK):
+            nc.vector.tensor_tensor(stg[:, t, :], bg[t][:], g3[t][:], ALU.subtract)
+        size = tile([P, PACK, W], F32, "size")
         for t in range(PACK):
             nc.scalar.activation(size[:, t, :], stg[:, t, :], ACT.Abs, scale=gb_inv[:, t : t + 1])
         logs = []
         for t in range(PACK):
-            tile = keep.tile([P, W], F32, name="log%d" % t)
-            nc.scalar.activation(tile[:], size[:, t, :], ACT.Ln, bias=0.5)
-            logs.append(tile)
-        inv = keep.tile([P, PACK, W], F32, name="inv")
-        for h in range(2):
+            rows = tile([P, W], F32, "log%d" % t, "g3%d" % (PACK - 1 - t))
+            nc.scalar.activation(rows[:], size[:, t, :], ACT.Ln, bias=0.5)
+            logs.append(rows)
+        parts = [(0, 256), (256, 384), (384, 512)]
+        inv = tile([P, PACK, W], F32, "inv", "size")
+        for a, b in parts:
             for t in range(PACK):
-                nc.scalar.activation(inv[:, t, cols(h)], logs[t][:].indirect(half(l_n4, h)), ACT.Exp, scale=-1.0)
+                nc.scalar.activation(inv[:, t, a:b], logs[t][:].indirect(entries(l_n4, a, b)), ACT.Exp, scale=-1.0)
 
+        za = tile([P, PACK, W], F32, "za")
+        zb = tile([P, PACK, W], F32, "zb")
         for t in range(PACK):
-            for h in range(2):
-                nc.vector.tensor_tensor(za[:, t, cols(h)], d[t][:].indirect(half(l_n2, h)), ya[t][:, cols(h)], ALU.mult)
-                nc.vector.tensor_tensor(zb[:, t, cols(h)], ya[t][:].indirect(half(l_n1, h)), d[t][:, cols(h)], ALU.mult)
+            for a, b in halves:
+                nc.vector.tensor_tensor(za[:, t, a:b], d[t][:].indirect(entries(l_n2, a, b)), ya[t][:, a:b], ALU.mult)
+                nc.vector.tensor_tensor(zb[:, t, a:b], ya[t][:].indirect(entries(l_n1, a, b)), d[t][:, a:b], ALU.mult)
 
-        def z_pair(h):
-            z_g = keep.tile([P, PACK * HALF], BF16, name="z_g%d" % h, align_bytes=64)
+        def z_tile(t, z_g):
             nc.vector.tensor_tensor(
-                z_g[:].rearrange("p (e m t) -> p m t e", e=2, t=PACK),
-                za[:].rearrange("p t (m h e) -> p h m t e", h=2, e=2)[:, h],
-                zb[:].rearrange("p t (m h e) -> p h m t e", h=2, e=2)[:, h],
+                z_g.rearrange("p (a e r) -> p a r e", e=2, r=PACK),
+                za[:].rearrange("p r (a t e) -> p t a r e", t=PACK, e=2)[:, t],
+                zb[:].rearrange("p r (a t e) -> p t a r e", t=PACK, e=2)[:, t],
                 ALU.subtract,
             )
-            return z_g
+            return quantize(z_g, P, "z_q%d" % t)
 
-        z2_c = keep.tile([P, W], U32, name="z2_c", align_bytes=64)
-        z2_s = keep.tile([P, W], U8, name="z2_s", align_bytes=64)
-
-        def z2_half(h):
-            part = keep.tile([P, PACK * HALF], BF16, name="z2_g%d" % h, align_bytes=64)
+        z_first = tile([P, W], BF16, "z_first")
+        z_q = [z_tile(0, z_first[:])]
+        z2_g = tile([P, PACK * W], BF16, "z2_g", "d3")
+        z2_c = tile([P, W], U32, "z2_c")
+        z2_s = tile([P, W], U8, "z2_s")
+        for a, b in parts:
+            part = z2_g[:, PACK * a : PACK * b]
             nc.vector.tensor_tensor(
-                part[:].rearrange("p (c i t) -> p c t i", i=2, t=PACK),
-                stg[:, :, cols(h)].rearrange("p t (c i) -> p c t i", i=2),
-                inv[:, :, cols(h)].rearrange("p t (c i) -> p c t i", i=2),
+                part.rearrange("p (c i t) -> p c t i", i=2, t=PACK),
+                stg[:, :, a:b].rearrange("p t (c i) -> p c t i", i=2),
+                inv[:, :, a:b].rearrange("p t (c i) -> p c t i", i=2),
                 ALU.mult,
             )
-            return part
+            nc.vector.quantize_mx(out=z2_c[:, a:b].bitcast(FP8X4), scales=z2_s[:, a:b], in_=part)
+        z_rest = tile([P, (PACK - 1) * W], BF16, "z_rest", "d3")
+        for t in range(1, PACK):
+            z_q.append(z_tile(t, z_rest[:, (t - 1) * W : t * W]))
 
-        def z2_quantize(part, h):
-            nc.vector.quantize_mx(out=z2_c[:, cols(h)].bitcast(FP8X4), scales=z2_s[:, cols(h)], in_=part[:])
-
-        z_g0 = z_pair(0)
-        z2_g0 = z2_half(0)
-        z_q = [quantize(z_g0, HALF, "z_q0")]
-        z2_quantize(z2_g0, 0)
-        z2_quantize(z2_half(1), 1)
-        z_q.append(quantize(z_pair(1), HALF, "z_q1"))
-
-        out_rows = out.rearrange("(p t) v -> p t v", t=PACK)
+        out_rows = out.rearrange("(a t e) v -> t e a v", t=PACK, e=2)
         for t in range(PACK):
-            acc = product(z_q[t // 2], (t % 2) * P, (z2_c, z2_s))
-            hs = keep.tile([P, W], F32, name="hs%d" % t)
+            acc = product(z_q[t], 0, (z2_c[:], z2_s[:]), 2)
+            hs = tile([P, W], F32, "hs%d" % t)
             nc.scalar.activation(hs[:], acc[:], ACT.Copy, scale=0.03125)
-            g5 = keep.tile([P, W], F32, name="g5%d" % t)
-            for h in range(2):
-                nc.scalar.activation(g5[:, cols(h)], hs[:].indirect(half(l_n5, h)), ACT.Copy, scale=2.0)
-            st2 = keep.tile([P, W], F32, name="st2%d" % t)
+            g5 = tile([P, W], F32, "g5%d" % t)
+            for a, b in halves:
+                nc.scalar.activation(g5[:, a:b], hs[:].indirect(entries(l_n5, a, b)), ACT.Copy, scale=2.0)
+            st2 = tile([P, W], F32, "st2%d" % t)
             nc.vector.scalar_tensor_tensor(st2[:], hs[:], 2.0, g5[:], ALU.mult, ALU.max)
-            res = keep.tile([P, W], F32, name="res%d" % t)
-            for h in range(2):
-                nc.vector.tensor_tensor(res[:, cols(h)], st2[:].indirect(half(l_n6, h)), hs[:, cols(h)], ALU.subtract)
-            nc.sync.dma_start(out_rows[:, t, :], res[:])
+            res = tile([P, W], F32, "res%d" % t)
+            for a, b in halves:
+                if (t, a) in [(3, HALF)]:
+                    g6 = tile([P, HALF], F32, "g6%d" % t)
+                    nc.scalar.activation(g6[:], st2[:].indirect(entries(l_n6, a, b)), ACT.Copy)
+                    nc.vector.tensor_tensor(res[:, a:b], g6[:], hs[:, a:b], ALU.subtract)
+                else:
+                    nc.vector.tensor_tensor(res[:, a:b], st2[:].indirect(entries(l_n6, a, b)), hs[:, a:b], ALU.subtract)
+                if t == PACK - 1:
+                    for e in range(2):
+                        nc.sync.dma_start(out_rows[t, e, :, a:b], res[e:P:2, a:b])
+            if t < PACK - 1:
+                for e in range(2):
+                    nc.sync.dma_start(out_rows[t, e], res[e:P:2, :])

@@ -69,6 +69,10 @@ def tile_picked_twkcrossbhopnhopb_none_p_kernel(tc, x_words, x_scales, w1, w2, w
         l_n5 = load_list(n5, "l_n5")
         l_n6 = load_list(n6, "l_n6")
 
+        warm = tile([P, 2], F32, "warm")
+        nc.gpsimd.memset(warm[:, 0:1], 1.0)
+        nc.scalar.activation(warm[:, 1:2], warm[:, 0:1], ACT.Ln)
+
         def pick_words(lst, name):
             words = tile([P, W], U32, name)
             nc.vector.tensor_copy(words[:], xw[:].bitcast(U32).indirect(lst[:]))

@@ -52,13 +52,13 @@ def tile_picked_twkcrossbhopnhopb_none_p_kernel(tc, x_words, x_scales, w1, w2, w
         nc.gpsimd.memset(xs[:, T // 2 :].bitcast(I32), 0)
         l_three = load_list(three, "l_three")
         l_offs = load_list(offs, "l_offs")
-        l_two = load_list(two, "l_two")
-        l_n3 = load_list(n3, "l_n3")
         xw = tile([P, T], I32, "xw")
         nc.sync.dma_start(xw[:], x_words[0].rearrange("p n t -> p (n t)").bitcast(I32))
         for q in range(4):
             nc.scalar.dma_start(xs[32 * q : 32 * q + 4, :].bitcast(I32), x_scales[0, 4 * q : 4 * q + 4, :].bitcast(I32))
         w3_raw = load_weight(w3, "w3_raw")
+        l_two = load_list(two, "l_two")
+        l_n3 = load_list(n3, "l_n3")
         w1_raw = load_weight(w1, "w1_raw")
         gb_t = load_rows(gb, "gb_t")
         w2_raw = load_weight(w2, "w2_raw")
@@ -133,8 +133,6 @@ def tile_picked_twkcrossbhopnhopb_none_p_kernel(tc, x_words, x_scales, w1, w2, w
         x12_s = tile([P, 2 * W], U8, "x12_s", "w3_raw")
         x1 = (x1_w, pick_scales(l_offs, x12_s[:, :W]))
 
-        ga75 = tile([P, PACK], F32, "ga75")
-        nc.vector.tensor_scalar(ga75[:], ga_t, 0.75, None, ALU.mult)
         gb_safe = tile([P, PACK], F32, "gb_safe")
         nc.vector.scalar_tensor_tensor(gb_safe[:], gb_t, 0.0, gb_t, ALU.is_equal, ALU.add)
         gb_inv = tile([P, PACK], F32, "gb_inv")
@@ -143,8 +141,8 @@ def tile_picked_twkcrossbhopnhopb_none_p_kernel(tc, x_words, x_scales, w1, w2, w
         bg = []
         for t in range(PACK):
             acc = product(w3_q[t // 2], (t % 2) * P, x3, t)
-            rows = tile([P, W], F32, "bg%d" % t)
-            nc.scalar.activation(rows[:], acc[:], ACT.Copy, scale=gb_t[:, t : t + 1])
+            rows = tile([P, 2 * W], F32, "bg%d" % t)
+            nc.scalar.activation(rows[:, :W], acc[:], ACT.Copy, scale=gb_t[:, t : t + 1])
             bg.append(rows)
 
         w1_g = weave(w1_raw, "w1_g")
@@ -155,27 +153,26 @@ def tile_picked_twkcrossbhopnhopb_none_p_kernel(tc, x_words, x_scales, w1, w2, w
         g3 = []
         for t in range(PACK):
             rows = tile([P, W], F32, "g3%d" % t)
-            for a, b in halves:
-                nc.scalar.activation(rows[:, a:b], bg[t][:].indirect(entries(l_n3, a, b)), ACT.Copy)
+            nc.scalar.activation(rows[:], bg[t][:].indirect(l_n3[:]), ACT.Copy)
             g3.append(rows)
 
         ya, d = [], []
         for t in range(PACK):
             acc = product(w1_q, t * P, x1, 4 + t)
-            rows = tile([P, W], F32, "ya%d" % t)
+            rows = tile([P, 2 * W], F32, "ya%d" % t)
             if t < 2:
-                nc.vector.tensor_scalar(rows[:], acc[:], ga75[:, t : t + 1], None, ALU.mult)
+                nc.vector.tensor_scalar(rows[:, :W], acc[:], ga_t[:, t : t + 1], None, ALU.mult)
             else:
-                nc.scalar.activation(rows[:], acc[:], ACT.Copy, scale=ga75[:, t : t + 1])
+                nc.scalar.activation(rows[:, :W], acc[:], ACT.Copy, scale=ga_t[:, t : t + 1])
             ya.append(rows)
             acc = product(w2_q, t * P, x2, (6 + t) % 8)
-            rows = tile([P, W], F32, "d%d" % t)
-            nc.scalar.copy(rows[:], acc[:])
+            rows = tile([P, 2 * W], F32, "d%d" % t)
+            nc.scalar.activation(rows[:, :W], acc[:], ACT.Copy, scale=0.75)
             d.append(rows)
 
         stg = tile([P, PACK, W], F32, "stg")
         for t in range(PACK):
-            nc.vector.tensor_tensor(stg[:, t, :], bg[t][:], g3[t][:], ALU.subtract)
+            nc.vector.tensor_tensor(stg[:, t, :], bg[t][:, :W], g3[t][:], ALU.subtract)
         size = tile([P, PACK, W], F32, "size")
         for t in range(PACK):
             nc.scalar.activation(size[:, t, :], stg[:, t, :], ACT.Abs, scale=gb_inv[:, t : t + 1])
@@ -193,9 +190,8 @@ def tile_picked_twkcrossbhopnhopb_none_p_kernel(tc, x_words, x_scales, w1, w2, w
         za = tile([P, PACK, W], F32, "za")
         zb = tile([P, PACK, W], F32, "zb")
         for t in range(PACK):
-            for a, b in halves:
-                nc.vector.tensor_tensor(za[:, t, a:b], d[t][:].indirect(entries(l_n2, a, b)), ya[t][:, a:b], ALU.mult)
-                nc.vector.tensor_tensor(zb[:, t, a:b], ya[t][:].indirect(entries(l_n1, a, b)), d[t][:, a:b], ALU.mult)
+            nc.vector.tensor_tensor(za[:, t, :], d[t][:].indirect(l_n2[:]), ya[t][:, :W], ALU.mult)
+            nc.vector.tensor_tensor(zb[:, t, :], ya[t][:].indirect(l_n1[:]), d[t][:, :W], ALU.mult)
 
         def z_tile(t, z_g):
             nc.vector.tensor_tensor(
@@ -227,24 +223,22 @@ def tile_picked_twkcrossbhopnhopb_none_p_kernel(tc, x_words, x_scales, w1, w2, w
         out_rows = out.rearrange("(a t e) v -> t e a v", t=PACK, e=2)
         for t in range(PACK):
             acc = product(z_q[t], 0, (z2_c[:], z2_s[:]), 2)
-            hs = tile([P, W], F32, "hs%d" % t)
-            nc.scalar.activation(hs[:], acc[:], ACT.Copy, scale=0.03125)
+            hs = tile([P, 2 * W], F32, "hs%d" % t)
+            nc.scalar.activation(hs[:, :W], acc[:], ACT.Copy, scale=0.03125)
             g5 = tile([P, W], F32, "g5%d" % t)
-            for a, b in halves:
-                nc.scalar.activation(g5[:, a:b], hs[:].indirect(entries(l_n5, a, b)), ACT.Copy, scale=2.0)
-            st2 = tile([P, W], F32, "st2%d" % t)
-            nc.vector.scalar_tensor_tensor(st2[:], hs[:], 2.0, g5[:], ALU.mult, ALU.max)
+            nc.scalar.activation(g5[:], hs[:].indirect(l_n5[:]), ACT.Copy, scale=2.0)
+            st2 = tile([P, 2 * W], F32, "st2%d" % t)
+            nc.vector.scalar_tensor_tensor(st2[:, :W], hs[:, :W], 2.0, g5[:], ALU.mult, ALU.max)
             res = tile([P, W], F32, "res%d" % t)
-            for a, b in halves:
-                if (t, a) in [(3, HALF)]:
-                    g6 = tile([P, HALF], F32, "g6%d" % t)
-                    nc.scalar.activation(g6[:], st2[:].indirect(entries(l_n6, a, b)), ACT.Copy)
-                    nc.vector.tensor_tensor(res[:, a:b], g6[:], hs[:, a:b], ALU.subtract)
-                else:
-                    nc.vector.tensor_tensor(res[:, a:b], st2[:].indirect(entries(l_n6, a, b)), hs[:, a:b], ALU.subtract)
-                if t == PACK - 1:
-                    for e in range(2):
-                        nc.sync.dma_start(out_rows[t, e, :, a:b], res[e:P:2, a:b])
             if t < PACK - 1:
+                nc.vector.tensor_tensor(res[:], st2[:].indirect(l_n6[:]), hs[:, :W], ALU.subtract)
                 for e in range(2):
                     nc.sync.dma_start(out_rows[t, e], res[e:P:2, :])
+            else:
+                g6 = tile([P, HALF], F32, "g6")
+                nc.scalar.activation(g6[:], st2[:].indirect(entries(l_n6, HALF, W)), ACT.Copy)
+                nc.vector.tensor_tensor(res[:, :HALF], st2[:].indirect(entries(l_n6, 0, HALF)), hs[:, :HALF], ALU.subtract)
+                nc.vector.tensor_tensor(res[:, HALF:], g6[:], hs[:, HALF:W], ALU.subtract)
+                for a, b in halves:
+                    for e in range(2):
+                        (nc.scalar if e else nc.sync).dma_start(out_rows[t, e, :, a:b], res[e:P:2, a:b])

@@ -14,25 +14,36 @@ ACT = mybir.ActivationFunctionType
 
 P = 128
 PACK = 4
-T = 2048
+TILES = 4
+TOKENS = 2048
 W = 512
 HALF = W // 2
+HALVES = [(0, HALF), (HALF, W)]
+WHOLE = [(0, W)]
+WIDE = 2 * W
+BANKS = 8
+
+Z2_PARTS = [(0, 256), (256, 384), (384, 512)]
+Y_TILES_ON_VECTOR = 2
+FIRST_SHARED_TILE = 2
 
 FLOPS = 4 * 2 * 512 * 512 * 512
 
 
-def tile_picked_twkcrossbhopnhopb_none_p_kernel(tc, x_words, x_scales, w1, w2, w3, ga, gb, offs, two, n1, n2, three, n3, n4, n5, n6, out):
+def tile_picked_twkcrossbhopnhopb_none_p_kernel(
+    tc, x_words, x_scales, w1, w2, w3, ga, gb, offs, two, n1, n2, three, n3, n4, n5, n6, out
+):
     nc = tc.nc
     with ExitStack() as ctx:
-        keep = ctx.enter_context(tc.tile_pool(name="keep", bufs=1))
+        lists = ctx.enter_context(tc.tile_pool(name="lists", bufs=1))
         work = ctx.enter_context(tc.tile_pool(name="work", bufs=1))
         psum = ctx.enter_context(tc.psum_pool(name="psum", bufs=1))
 
-        def tile(shape, dtype, name, tag=None):
-            return work.tile(shape, dtype, name=name, tag=tag or name, align_bytes=64)
+        def tile(shape, dtype, name, takes_over=None):
+            return work.tile(shape, dtype, name=name, tag=takes_over or name, align_bytes=64)
 
         def load_list(src, name):
-            lst = keep.tile([P, W // 16], U16, name=name)
+            lst = lists.tile([P, W // 16], U16, name=name)
             nc.sync.dma_start(lst[:], src)
             return lst
 
@@ -41,204 +52,218 @@ def tile_picked_twkcrossbhopnhopb_none_p_kernel(tc, x_words, x_scales, w1, w2, w
             nc.sync.dma_start(raw[:], src.rearrange("(p j) c -> p j c", j=PACK))
             return raw
 
-        def load_rows(src, name):
-            rows = tile([P, 7], F32, name)
+        def load_row_factors(src, name):
+            run = 2 * TILES - 1
+            runs = tile([P, run], F32, name)
             for e in range(2):
-                nc.sync.dma_start(rows[e:P:2, :], src.rearrange("(a c) o -> a (c o)", c=8)[:, e : e + 7])
-            return rows[:, 0:7:2]
+                nc.sync.dma_start(runs[e:P:2, :], src.rearrange("(a c) o -> a (c o)", c=2 * TILES)[:, e : e + run])
+            return runs[:, 0:run:2]
 
-        xs = tile([P, T], U8, "xs")
-        nc.vector.memset(xs[:, : T // 2].bitcast(I32), 0)
-        nc.gpsimd.memset(xs[:, T // 2 :].bitcast(I32), 0)
-        l_three = load_list(three, "l_three")
-        l_offs = load_list(offs, "l_offs")
-        xw = tile([P, T], I32, "xw")
-        nc.sync.dma_start(xw[:], x_words[0].rearrange("p n t -> p (n t)").bitcast(I32))
-        for q in range(4):
-            nc.scalar.dma_start(xs[32 * q : 32 * q + 4, :].bitcast(I32), x_scales[0, 4 * q : 4 * q + 4, :].bitcast(I32))
-        w3_raw = load_weight(w3, "w3_raw")
-        l_two = load_list(two, "l_two")
-        l_n3 = load_list(n3, "l_n3")
-        w1_raw = load_weight(w1, "w1_raw")
-        gb_t = load_rows(gb, "gb_t")
-        w2_raw = load_weight(w2, "w2_raw")
-        ga_t = load_rows(ga, "ga_t")
-        l_n1 = load_list(n1, "l_n1")
-        l_n2 = load_list(n2, "l_n2")
-        l_n4 = load_list(n4, "l_n4")
-        l_n5 = load_list(n5, "l_n5")
-        l_n6 = load_list(n6, "l_n6")
-
-        warm = tile([P, 2], F32, "warm")
-        nc.gpsimd.memset(warm[:, 0:1], 1.0)
-        nc.scalar.activation(warm[:, 1:2], warm[:, 0:1], ACT.Ln)
+        def entries(lst, first, end):
+            return lst[:, first // 16 : end // 16]
 
         def pick_words(lst, name):
             words = tile([P, W], U32, name)
-            nc.vector.tensor_copy(words[:], xw[:].bitcast(U32).indirect(lst[:]))
+            nc.vector.tensor_copy(words[:], table_words[:].bitcast(U32).indirect(lst[:]))
             return words[:]
 
-        def pick_scales(lst, dst):
-            nc.vector.tensor_copy(dst, xs[:].indirect(lst[:]))
-            return dst
+        def pick_scales(lst, scales):
+            nc.vector.tensor_copy(scales, table_scales[:].indirect(lst[:]))
+            return scales
 
-        def quantize(grouped, width, name):
-            codes = tile([P, width], U32, name + "_c")
-            scales = tile([P, width], U8, name + "_s")
-            nc.vector.quantize_mx(out=codes[:].bitcast(FP8X4), scales=scales[:], in_=grouped)
+        def weave(raw, name):
+            woven = tile([P, PACK * W], BF16, name, "woven")
+            nc.vector.tensor_copy(
+                woven[:].rearrange("p (t a e j) -> p a t j e", t=TILES, e=2, j=PACK),
+                raw[:].rearrange("p j (a t e) -> p a t j e", t=TILES, e=2),
+            )
+            return woven
+
+        def quantize(woven, columns, name):
+            codes = tile([P, columns], U32, name + "_codes")
+            scales = tile([P, columns], U8, name + "_scales")
+            nc.vector.quantize_mx(out=codes[:].bitcast(FP8X4), scales=scales[:], in_=woven)
             return codes, scales
 
-        def product(lhs, col, rhs, bank):
-            acc = psum.tile([P, W], F32, name="acc", tag="bank%d" % bank)
+        def product(stationary, column, moving, bank):
+            acc = psum.tile([P, moving[1].shape[1]], F32, name="acc", tag="bank%d" % bank)
             nc.tensor.matmul_mx(
                 out=acc[:],
-                lhsT=lhs[0][:, col : col + P].bitcast(FP8X4),
-                lhsT_scale=lhs[1][:, col : col + P],
-                rhs=rhs[0].bitcast(FP8X4),
-                rhs_scale=rhs[1],
+                lhsT=stationary[0][:, column : column + P].bitcast(FP8X4),
+                lhsT_scale=stationary[1][:, column : column + P],
+                rhs=moving[0].bitcast(FP8X4),
+                rhs_scale=moving[1],
                 start=True,
                 stop=True,
             )
             return acc
 
-        def entries(lst, a, b):
-            return lst[:, a // 16 : b // 16]
-
-        halves = [(0, HALF), (HALF, W)]
-
-        def weave(raw, name):
-            grouped = tile([P, PACK * W], BF16, name, "grouped")
-            nc.vector.tensor_copy(
-                grouped[:].rearrange("p (t a e j) -> p a t j e", t=PACK, e=2, j=PACK),
-                raw[:].rearrange("p j (a t e) -> p a t j e", t=PACK, e=2),
+        table_scales = tile([P, TOKENS], U8, "table_scales")
+        nc.vector.memset(table_scales[:, : TOKENS // 2].bitcast(I32), 0)
+        nc.gpsimd.memset(table_scales[:, TOKENS // 2 :].bitcast(I32), 0)
+        list_three = load_list(three, "list_three")
+        table_words = tile([P, TOKENS], I32, "table_words")
+        nc.sync.dma_start(table_words[:], x_words[0].rearrange("p n t -> p (n t)").bitcast(I32))
+        list_offs = load_list(offs, "list_offs")
+        for q in range(4):
+            nc.scalar.dma_start(
+                table_scales[32 * q : 32 * q + 4, :].bitcast(I32), x_scales[0, 4 * q : 4 * q + 4, :].bitcast(I32)
             )
-            return grouped
+        w3_raw = load_weight(w3, "w3_raw")
+        list_two = load_list(two, "list_two")
+        list_n3 = load_list(n3, "list_n3")
+        w1_raw = load_weight(w1, "w1_raw")
+        gb_rows = load_row_factors(gb, "gb_rows")
+        w2_raw = load_weight(w2, "w2_raw")
+        ga_rows = load_row_factors(ga, "ga_rows")
+        list_n1 = load_list(n1, "list_n1")
+        list_n2 = load_list(n2, "list_n2")
+        list_n4 = load_list(n4, "list_n4")
+        list_n5 = load_list(n5, "list_n5")
+        list_n6 = load_list(n6, "list_n6")
 
-        x3_w = pick_words(l_three, "x3_w")
-        x3_s = tile([P, W], U8, "x3_s")
-        x3 = (x3_w, pick_scales(l_three, x3_s[:]))
-        w3_g = []
-        for h in range(2):
-            grouped = tile([P, PACK * HALF], BF16, "w3_g%d" % h, "grouped" if h else None)
+        warm = tile([P, 2], F32, "warm")
+        nc.gpsimd.memset(warm[:, 0:1], 1.0)
+        nc.scalar.activation(warm[:, 1:2], warm[:, 0:1], ACT.Ln)
+
+        x3_words = pick_words(list_three, "x3_words")
+        x3_scales = tile([P, W], U8, "x3_scales")
+        x3 = (x3_words, pick_scales(list_three, x3_scales[:]))
+        w3_woven = []
+        for pair in range(2):
+            woven = tile([P, PACK * HALF], BF16, "w3_woven%d" % pair, "woven" if pair else None)
             for u in range(2):
                 nc.scalar.activation(
-                    grouped[:].rearrange("p (u a e j) -> p u a j e", u=2, e=2, j=PACK)[:, u],
-                    w3_raw[:].rearrange("p j (a t e) -> p t a j e", t=PACK, e=2)[:, 2 * h + u],
+                    woven[:].rearrange("p (u a e j) -> p u a j e", u=2, e=2, j=PACK)[:, u],
+                    w3_raw[:].rearrange("p j (a t e) -> p t a j e", t=TILES, e=2)[:, 2 * pair + u],
                     ACT.Copy,
                 )
-            w3_g.append(grouped)
-        x1_w = pick_words(l_offs, "x1_w")
-        x2_w = pick_words(l_two, "x2_w")
-        w3_q = [quantize(w3_g[h][:], HALF, "w3_q%d" % h) for h in range(2)]
-        x12_s = tile([P, 2 * W], U8, "x12_s", "w3_raw")
-        x1 = (x1_w, pick_scales(l_offs, x12_s[:, :W]))
+            w3_woven.append(woven)
+        x1_words = pick_words(list_offs, "x1_words")
+        x2_words = pick_words(list_two, "x2_words")
+        w3_q = [quantize(w3_woven[pair][:], HALF, "w3_q%d" % pair) for pair in range(2)]
+        x12_scales = tile([P, 2 * W], U8, "x12_scales", "w3_raw")
+        x1 = (x1_words, pick_scales(list_offs, x12_scales[:, :W]))
 
-        gb_safe = tile([P, PACK], F32, "gb_safe")
-        nc.vector.scalar_tensor_tensor(gb_safe[:], gb_t, 0.0, gb_t, ALU.is_equal, ALU.add)
-        gb_inv = tile([P, PACK], F32, "gb_inv")
-        nc.vector.reciprocal(gb_inv[:], gb_safe[:])
+        gb_nonzero = tile([P, TILES], F32, "gb_nonzero")
+        nc.vector.scalar_tensor_tensor(gb_nonzero[:], gb_rows, 0.0, gb_rows, ALU.is_equal, ALU.add)
+        gb_inverse = tile([P, TILES], F32, "gb_inverse")
+        nc.vector.reciprocal(gb_inverse[:], gb_nonzero[:])
 
-        bg = []
-        for t in range(PACK):
+        gb_b = []
+        for t in range(TILES):
             acc = product(w3_q[t // 2], (t % 2) * P, x3, t)
-            rows = tile([P, 2 * W], F32, "bg%d" % t)
-            nc.scalar.activation(rows[:, :W], acc[:], ACT.Copy, scale=gb_t[:, t : t + 1])
-            bg.append(rows)
+            rows = tile([P, WIDE], F32, "gb_b%d" % t)
+            nc.scalar.activation(rows[:, :W], acc[:], ACT.Copy, scale=gb_rows[:, t : t + 1])
+            gb_b.append(rows)
 
-        w1_g = weave(w1_raw, "w1_g")
-        x2 = (x2_w, pick_scales(l_two, x12_s[:, W:]))
-        w1_q = quantize(w1_g[:], W, "w1_q")
-        w2_q = quantize(weave(w2_raw, "w2_g")[:], W, "w2_q")
+        w1_woven = weave(w1_raw, "w1_woven")
+        x2 = (x2_words, pick_scales(list_two, x12_scales[:, W:]))
+        w1_q = quantize(w1_woven[:], W, "w1_q")
+        w2_q = quantize(weave(w2_raw, "w2_woven")[:], W, "w2_q")
 
-        g3 = []
-        for t in range(PACK):
-            rows = tile([P, W], F32, "g3%d" % t)
-            nc.scalar.activation(rows[:], bg[t][:].indirect(l_n3[:]), ACT.Copy)
-            g3.append(rows)
+        gb_b_n3 = []
+        for t in range(TILES):
+            rows = tile([P, W], F32, "gb_b_n3_%d" % t)
+            nc.scalar.activation(rows[:], gb_b[t][:].indirect(list_n3[:]), ACT.Copy)
+            gb_b_n3.append(rows)
 
-        ya, d = [], []
-        for t in range(PACK):
-            acc = product(w1_q, t * P, x1, 4 + t)
-            rows = tile([P, 2 * W], F32, "ya%d" % t)
-            if t < 2:
-                nc.vector.tensor_scalar(rows[:, :W], acc[:], ga_t[:, t : t + 1], None, ALU.mult)
+        ga_y, d75 = [], []
+        for t in range(TILES):
+            acc = product(w1_q, t * P, x1, TILES + t)
+            rows = tile([P, WIDE], F32, "ga_y%d" % t)
+            if t < Y_TILES_ON_VECTOR:
+                nc.vector.tensor_scalar(rows[:, :W], acc[:], ga_rows[:, t : t + 1], None, ALU.mult)
             else:
-                nc.scalar.activation(rows[:, :W], acc[:], ACT.Copy, scale=ga_t[:, t : t + 1])
-            ya.append(rows)
-            acc = product(w2_q, t * P, x2, (6 + t) % 8)
-            rows = tile([P, 2 * W], F32, "d%d" % t)
+                nc.scalar.activation(rows[:, :W], acc[:], ACT.Copy, scale=ga_rows[:, t : t + 1])
+            ga_y.append(rows)
+            acc = product(w2_q, t * P, x2, (TILES + t + 2) % BANKS)
+            rows = tile([P, WIDE], F32, "d75_%d" % t)
             nc.scalar.activation(rows[:, :W], acc[:], ACT.Copy, scale=0.75)
-            d.append(rows)
+            d75.append(rows)
+        last_d75 = "d75_%d" % (TILES - 1)
 
-        stg = tile([P, PACK, W], F32, "stg")
-        for t in range(PACK):
-            nc.vector.tensor_tensor(stg[:, t, :], bg[t][:, :W], g3[t][:], ALU.subtract)
-        size = tile([P, PACK, W], F32, "size")
-        for t in range(PACK):
-            nc.scalar.activation(size[:, t, :], stg[:, t, :], ACT.Abs, scale=gb_inv[:, t : t + 1])
+        gb_st = tile([P, TILES, W], F32, "gb_st")
+        for t in range(TILES):
+            nc.vector.tensor_tensor(gb_st[:, t, :], gb_b[t][:, :W], gb_b_n3[t][:], ALU.subtract)
+        abs_st = tile([P, TILES, W], F32, "abs_st")
+        for t in range(TILES):
+            nc.scalar.activation(abs_st[:, t, :], gb_st[:, t, :], ACT.Abs, scale=gb_inverse[:, t : t + 1])
         logs = []
-        for t in range(PACK):
-            rows = tile([P, W], F32, "log%d" % t, "g3%d" % (PACK - 1 - t))
-            nc.scalar.activation(rows[:], size[:, t, :], ACT.Ln, bias=0.5)
+        for t in range(TILES):
+            rows = tile([P, W], F32, "log%d" % t, "gb_b_n3_%d" % (TILES - 1 - t))
+            nc.scalar.activation(rows[:], abs_st[:, t, :], ACT.Ln, bias=0.5)
             logs.append(rows)
-        parts = [(0, 256), (256, 384), (384, 512)]
-        inv = tile([P, PACK, W], F32, "inv", "size")
-        for a, b in parts:
-            for t in range(PACK):
-                nc.scalar.activation(inv[:, t, a:b], logs[t][:].indirect(entries(l_n4, a, b)), ACT.Exp, scale=-1.0)
+        reciprocal = tile([P, TILES, W], F32, "reciprocal", "abs_st")
+        for first, end in Z2_PARTS:
+            for t in range(TILES):
+                nc.scalar.activation(
+                    reciprocal[:, t, first:end], logs[t][:].indirect(entries(list_n4, first, end)), ACT.Exp, scale=-1.0
+                )
 
-        za = tile([P, PACK, W], F32, "za")
-        zb = tile([P, PACK, W], F32, "zb")
-        for t in range(PACK):
-            nc.vector.tensor_tensor(za[:, t, :], d[t][:].indirect(l_n2[:]), ya[t][:, :W], ALU.mult)
-            nc.vector.tensor_tensor(zb[:, t, :], ya[t][:].indirect(l_n1[:]), d[t][:, :W], ALU.mult)
+        z_plus = tile([P, TILES, W], F32, "z_plus")
+        z_minus = tile([P, TILES, W], F32, "z_minus")
+        for t in range(TILES):
+            nc.vector.tensor_tensor(z_plus[:, t, :], d75[t][:].indirect(list_n2[:]), ga_y[t][:, :W], ALU.mult)
+            nc.vector.tensor_tensor(z_minus[:, t, :], ga_y[t][:].indirect(list_n1[:]), d75[t][:, :W], ALU.mult)
 
-        def z_tile(t, z_g):
+        def z_columns(t, woven):
             nc.vector.tensor_tensor(
-                z_g.rearrange("p (a e r) -> p a r e", e=2, r=PACK),
-                za[:].rearrange("p r (a t e) -> p t a r e", t=PACK, e=2)[:, t],
-                zb[:].rearrange("p r (a t e) -> p t a r e", t=PACK, e=2)[:, t],
+                woven.rearrange("p (a e r) -> p a r e", e=2, r=TILES),
+                z_plus[:].rearrange("p r (a t e) -> p t a r e", t=TILES, e=2)[:, t],
+                z_minus[:].rearrange("p r (a t e) -> p t a r e", t=TILES, e=2)[:, t],
                 ALU.subtract,
             )
-            return quantize(z_g, P, "z_q%d" % t)
+            return quantize(woven, P, "z_q%d" % t)
 
         z_first = tile([P, W], BF16, "z_first")
-        z_q = [z_tile(0, z_first[:])]
-        z2_g = tile([P, PACK * W], BF16, "z2_g", "d3")
-        z2_c = tile([P, W], U32, "z2_c")
-        z2_s = tile([P, W], U8, "z2_s")
-        for a, b in parts:
-            part = z2_g[:, PACK * a : PACK * b]
+        z_q = [z_columns(0, z_first[:])]
+        z2_woven = tile([P, PACK * W], BF16, "z2_woven", last_d75)
+        z2_codes = tile([P, W], U32, "z2_codes")
+        z2_scales = tile([P, W], U8, "z2_scales")
+        for first, end in Z2_PARTS:
+            woven = z2_woven[:, PACK * first : PACK * end]
             nc.vector.tensor_tensor(
-                part.rearrange("p (c i t) -> p c t i", i=2, t=PACK),
-                stg[:, :, a:b].rearrange("p t (c i) -> p c t i", i=2),
-                inv[:, :, a:b].rearrange("p t (c i) -> p c t i", i=2),
+                woven.rearrange("p (c e r) -> p c r e", e=2, r=TILES),
+                gb_st[:, :, first:end].rearrange("p r (c e) -> p c r e", e=2),
+                reciprocal[:, :, first:end].rearrange("p r (c e) -> p c r e", e=2),
                 ALU.mult,
             )
-            nc.vector.quantize_mx(out=z2_c[:, a:b].bitcast(FP8X4), scales=z2_s[:, a:b], in_=part)
-        z_rest = tile([P, (PACK - 1) * W], BF16, "z_rest", "d3")
-        for t in range(1, PACK):
-            z_q.append(z_tile(t, z_rest[:, (t - 1) * W : t * W]))
+            nc.vector.quantize_mx(out=z2_codes[:, first:end].bitcast(FP8X4), scales=z2_scales[:, first:end], in_=woven)
+        z_rest = tile([P, (TILES - 1) * W], BF16, "z_rest", last_d75)
+        for t in range(1, TILES):
+            z_q.append(z_columns(t, z_rest[:, (t - 1) * W : t * W]))
 
-        out_rows = out.rearrange("(a t e) v -> t e a v", t=PACK, e=2)
-        for t in range(PACK):
-            acc = product(z_q[t], 0, (z2_c[:], z2_s[:]), 2)
-            hs = tile([P, 2 * W], F32, "hs%d" % t)
-            nc.scalar.activation(hs[:, :W], acc[:], ACT.Copy, scale=0.03125)
-            g5 = tile([P, W], F32, "g5%d" % t)
-            nc.scalar.activation(g5[:], hs[:].indirect(l_n5[:]), ACT.Copy, scale=2.0)
-            st2 = tile([P, 2 * W], F32, "st2%d" % t)
-            nc.vector.scalar_tensor_tensor(st2[:, :W], hs[:, :W], 2.0, g5[:], ALU.mult, ALU.max)
-            res = tile([P, W], F32, "res%d" % t)
-            if t < PACK - 1:
-                nc.vector.tensor_tensor(res[:], st2[:].indirect(l_n6[:]), hs[:, :W], ALU.subtract)
+        out_rows = out.rearrange("(a t e) v -> t e a v", t=TILES, e=2)
+        for t in range(TILES):
+            last = t == TILES - 1
+            half_s = tile([P, WIDE], F32, "half_s%d" % t)
+            parts = Z2_PARTS if t == 0 else WHOLE
+            for n, (first, end) in enumerate(parts):
+                acc = product(z_q[t], 0, (z2_codes[:, first:end], z2_scales[:, first:end]), len(parts) - 1 - n)
+                nc.scalar.activation(half_s[:, first:end], acc[:], ACT.Copy, scale=0.03125)
+            s_n5 = tile([P, W], F32, "s_n5_%d" % t)
+            st2 = tile([P, WIDE], F32, "st2_%d" % t)
+            for first, end in HALVES if last else WHOLE:
+                nc.scalar.activation(
+                    s_n5[:, first:end], half_s[:].indirect(entries(list_n5, first, end)), ACT.Copy, scale=2.0
+                )
+                nc.vector.scalar_tensor_tensor(
+                    st2[:, first:end], half_s[:, first:end], 2.0, s_n5[:, first:end], ALU.mult, ALU.max
+                )
+            result = tile([P, W], F32, "result%d" % t)
+            if t < FIRST_SHARED_TILE:
+                nc.vector.tensor_tensor(result[:], st2[:].indirect(list_n6[:]), half_s[:, :W], ALU.subtract)
                 for e in range(2):
-                    nc.sync.dma_start(out_rows[t, e], res[e:P:2, :])
+                    nc.sync.dma_start(out_rows[t, e], result[e:P:2, :])
             else:
-                g6 = tile([P, HALF], F32, "g6")
-                nc.scalar.activation(g6[:], st2[:].indirect(entries(l_n6, HALF, W)), ACT.Copy)
-                nc.vector.tensor_tensor(res[:, :HALF], st2[:].indirect(entries(l_n6, 0, HALF)), hs[:, :HALF], ALU.subtract)
-                nc.vector.tensor_tensor(res[:, HALF:], g6[:], hs[:, HALF:W], ALU.subtract)
-                for a, b in halves:
+                st2_n6 = tile([P, HALF], F32, "st2_n6_%d" % t)
+                nc.scalar.activation(st2_n6[:], st2[:].indirect(entries(list_n6, HALF, W)), ACT.Copy)
+                nc.vector.tensor_tensor(
+                    result[:, :HALF], st2[:].indirect(entries(list_n6, 0, HALF)), half_s[:, :HALF], ALU.subtract
+                )
+                nc.vector.tensor_tensor(result[:, HALF:], st2_n6[:], half_s[:, HALF:W], ALU.subtract)
+                for first, end in HALVES:
                     for e in range(2):
-                        (nc.scalar if e else nc.sync).dma_start(out_rows[t, e, :, a:b], res[e:P:2, a:b])
+                        queue = nc.scalar if e and last else nc.sync
+                        queue.dma_start(out_rows[t, e, :, first:end], result[e:P:2, first:end])

from contextlib import ExitStack

import concourse.mybir as mybir

F32 = mybir.dt.float32
BF16 = mybir.dt.bfloat16
I32 = mybir.dt.int32
U32 = mybir.dt.uint32
U16 = mybir.dt.uint16
U8 = mybir.dt.uint8
FP8X4 = mybir.dt.float8_e4m3fn_x4
ALU = mybir.AluOpType
ACT = mybir.ActivationFunctionType

P = 128
PACK = 4
TILES = 4
TOKENS = 2048
W = 512
HALF = W // 2
HALVES = [(0, HALF), (HALF, W)]
WHOLE = [(0, W)]
WIDE = 2 * W
BANKS = 8

Z2_PARTS = [(0, 256), (256, 384), (384, 512)]
Y_TILES_ON_VECTOR = 2
FIRST_SHARED_TILE = 2

FLOPS = 4 * 2 * 512 * 512 * 512


def tile_picked_twkcrossbhopnhopb_none_p_kernel(
    tc, x_words, x_scales, w1, w2, w3, ga, gb, offs, two, n1, n2, three, n3, n4, n5, n6, out
):
    nc = tc.nc
    with ExitStack() as ctx:
        lists = ctx.enter_context(tc.tile_pool(name="lists", bufs=1))
        work = ctx.enter_context(tc.tile_pool(name="work", bufs=1))
        psum = ctx.enter_context(tc.psum_pool(name="psum", bufs=1))

        def tile(shape, dtype, name, takes_over=None):
            return work.tile(shape, dtype, name=name, tag=takes_over or name, align_bytes=64)

        def load_list(src, name):
            lst = lists.tile([P, W // 16], U16, name=name)
            nc.sync.dma_start(lst[:], src)
            return lst

        def load_weight(src, name):
            raw = tile([P, PACK, W], F32, name)
            nc.sync.dma_start(raw[:], src.rearrange("(p j) c -> p j c", j=PACK))
            return raw

        def load_row_factors(src, name):
            run = 2 * TILES - 1
            runs = tile([P, run], F32, name)
            for e in range(2):
                nc.sync.dma_start(runs[e:P:2, :], src.rearrange("(a c) o -> a (c o)", c=2 * TILES)[:, e : e + run])
            return runs[:, 0:run:2]

        def entries(lst, first, end):
            return lst[:, first // 16 : end // 16]

        def pick_words(lst, name):
            words = tile([P, W], U32, name)
            nc.vector.tensor_copy(words[:], table_words[:].bitcast(U32).indirect(lst[:]))
            return words[:]

        def pick_scales(lst, scales):
            nc.vector.tensor_copy(scales, table_scales[:].indirect(lst[:]))
            return scales

        def weave(raw, name):
            woven = tile([P, PACK * W], BF16, name, "woven")
            nc.vector.tensor_copy(
                woven[:].rearrange("p (t a e j) -> p a t j e", t=TILES, e=2, j=PACK),
                raw[:].rearrange("p j (a t e) -> p a t j e", t=TILES, e=2),
            )
            return woven

        def quantize(woven, columns, name):
            codes = tile([P, columns], U32, name + "_codes")
            scales = tile([P, columns], U8, name + "_scales")
            nc.vector.quantize_mx(out=codes[:].bitcast(FP8X4), scales=scales[:], in_=woven)
            return codes, scales

        def product(stationary, column, moving, bank):
            acc = psum.tile([P, moving[1].shape[1]], F32, name="acc", tag="bank%d" % bank)
            nc.tensor.matmul_mx(
                out=acc[:],
                lhsT=stationary[0][:, column : column + P].bitcast(FP8X4),
                lhsT_scale=stationary[1][:, column : column + P],
                rhs=moving[0].bitcast(FP8X4),
                rhs_scale=moving[1],
                start=True,
                stop=True,
            )
            return acc

        table_scales = tile([P, TOKENS], U8, "table_scales")
        nc.vector.memset(table_scales[:, : TOKENS // 2].bitcast(I32), 0)
        nc.gpsimd.memset(table_scales[:, TOKENS // 2 :].bitcast(I32), 0)
        list_three = load_list(three, "list_three")
        table_words = tile([P, TOKENS], I32, "table_words")
        nc.sync.dma_start(table_words[:], x_words[0].rearrange("p n t -> p (n t)").bitcast(I32))
        list_offs = load_list(offs, "list_offs")
        for q in range(4):
            nc.scalar.dma_start(
                table_scales[32 * q : 32 * q + 4, :].bitcast(I32), x_scales[0, 4 * q : 4 * q + 4, :].bitcast(I32)
            )
        w3_raw = load_weight(w3, "w3_raw")
        list_two = load_list(two, "list_two")
        list_n3 = load_list(n3, "list_n3")
        w1_raw = load_weight(w1, "w1_raw")
        gb_rows = load_row_factors(gb, "gb_rows")
        w2_raw = load_weight(w2, "w2_raw")
        ga_rows = load_row_factors(ga, "ga_rows")
        list_n1 = load_list(n1, "list_n1")
        list_n2 = load_list(n2, "list_n2")
        list_n4 = load_list(n4, "list_n4")
        list_n5 = load_list(n5, "list_n5")
        list_n6 = load_list(n6, "list_n6")

        warm = tile([P, 2], F32, "warm")
        nc.gpsimd.memset(warm[:, 0:1], 1.0)
        nc.scalar.activation(warm[:, 1:2], warm[:, 0:1], ACT.Ln)

        x3_words = pick_words(list_three, "x3_words")
        x3_scales = tile([P, W], U8, "x3_scales")
        x3 = (x3_words, pick_scales(list_three, x3_scales[:]))
        w3_woven = []
        for pair in range(2):
            woven = tile([P, PACK * HALF], BF16, "w3_woven%d" % pair, "woven" if pair else None)
            for u in range(2):
                nc.scalar.activation(
                    woven[:].rearrange("p (u a e j) -> p u a j e", u=2, e=2, j=PACK)[:, u],
                    w3_raw[:].rearrange("p j (a t e) -> p t a j e", t=TILES, e=2)[:, 2 * pair + u],
                    ACT.Copy,
                )
            w3_woven.append(woven)
        x1_words = pick_words(list_offs, "x1_words")
        x2_words = pick_words(list_two, "x2_words")
        w3_q = [quantize(w3_woven[pair][:], HALF, "w3_q%d" % pair) for pair in range(2)]
        x12_scales = tile([P, 2 * W], U8, "x12_scales", "w3_raw")
        x1 = (x1_words, pick_scales(list_offs, x12_scales[:, :W]))

        gb_nonzero = tile([P, TILES], F32, "gb_nonzero")
        nc.vector.scalar_tensor_tensor(gb_nonzero[:], gb_rows, 0.0, gb_rows, ALU.is_equal, ALU.add)
        gb_inverse = tile([P, TILES], F32, "gb_inverse")
        nc.vector.reciprocal(gb_inverse[:], gb_nonzero[:])

        gb_b = []
        for t in range(TILES):
            acc = product(w3_q[t // 2], (t % 2) * P, x3, t)
            rows = tile([P, WIDE], F32, "gb_b%d" % t)
            nc.scalar.activation(rows[:, :W], acc[:], ACT.Copy, scale=gb_rows[:, t : t + 1])
            gb_b.append(rows)

        w1_woven = weave(w1_raw, "w1_woven")
        x2 = (x2_words, pick_scales(list_two, x12_scales[:, W:]))
        w1_q = quantize(w1_woven[:], W, "w1_q")
        w2_q = quantize(weave(w2_raw, "w2_woven")[:], W, "w2_q")

        gb_b_n3 = []
        for t in range(TILES):
            rows = tile([P, W], F32, "gb_b_n3_%d" % t)
            nc.scalar.activation(rows[:], gb_b[t][:].indirect(list_n3[:]), ACT.Copy)
            gb_b_n3.append(rows)

        ga_y, d75 = [], []
        for t in range(TILES):
            acc = product(w1_q, t * P, x1, TILES + t)
            rows = tile([P, WIDE], F32, "ga_y%d" % t)
            if t < Y_TILES_ON_VECTOR:
                nc.vector.tensor_scalar(rows[:, :W], acc[:], ga_rows[:, t : t + 1], None, ALU.mult)
            else:
                nc.scalar.activation(rows[:, :W], acc[:], ACT.Copy, scale=ga_rows[:, t : t + 1])
            ga_y.append(rows)
            acc = product(w2_q, t * P, x2, (TILES + t + 2) % BANKS)
            rows = tile([P, WIDE], F32, "d75_%d" % t)
            nc.scalar.activation(rows[:, :W], acc[:], ACT.Copy, scale=0.75)
            d75.append(rows)
        last_d75 = "d75_%d" % (TILES - 1)

        gb_st = tile([P, TILES, W], F32, "gb_st")
        for t in range(TILES):
            nc.vector.tensor_tensor(gb_st[:, t, :], gb_b[t][:, :W], gb_b_n3[t][:], ALU.subtract)
        abs_st = tile([P, TILES, W], F32, "abs_st")
        for t in range(TILES):
            nc.scalar.activation(abs_st[:, t, :], gb_st[:, t, :], ACT.Abs, scale=gb_inverse[:, t : t + 1])
        logs = []
        for t in range(TILES):
            rows = tile([P, W], F32, "log%d" % t, "gb_b_n3_%d" % (TILES - 1 - t))
            nc.scalar.activation(rows[:], abs_st[:, t, :], ACT.Ln, bias=0.5)
            logs.append(rows)
        reciprocal = tile([P, TILES, W], F32, "reciprocal", "abs_st")
        for first, end in Z2_PARTS:
            for t in range(TILES):
                nc.scalar.activation(
                    reciprocal[:, t, first:end], logs[t][:].indirect(entries(list_n4, first, end)), ACT.Exp, scale=-1.0
                )

        z_plus = tile([P, TILES, W], F32, "z_plus")
        z_minus = tile([P, TILES, W], F32, "z_minus")
        for t in range(TILES):
            nc.vector.tensor_tensor(z_plus[:, t, :], d75[t][:].indirect(list_n2[:]), ga_y[t][:, :W], ALU.mult)
            nc.vector.tensor_tensor(z_minus[:, t, :], ga_y[t][:].indirect(list_n1[:]), d75[t][:, :W], ALU.mult)

        def z_columns(t, woven):
            nc.vector.tensor_tensor(
                woven.rearrange("p (a e r) -> p a r e", e=2, r=TILES),
                z_plus[:].rearrange("p r (a t e) -> p t a r e", t=TILES, e=2)[:, t],
                z_minus[:].rearrange("p r (a t e) -> p t a r e", t=TILES, e=2)[:, t],
                ALU.subtract,
            )
            return quantize(woven, P, "z_q%d" % t)

        z_first = tile([P, W], BF16, "z_first")
        z_q = [z_columns(0, z_first[:])]
        z2_woven = tile([P, PACK * W], BF16, "z2_woven", last_d75)
        z2_codes = tile([P, W], U32, "z2_codes")
        z2_scales = tile([P, W], U8, "z2_scales")
        for first, end in Z2_PARTS:
            woven = z2_woven[:, PACK * first : PACK * end]
            nc.vector.tensor_tensor(
                woven.rearrange("p (c e r) -> p c r e", e=2, r=TILES),
                gb_st[:, :, first:end].rearrange("p r (c e) -> p c r e", e=2),
                reciprocal[:, :, first:end].rearrange("p r (c e) -> p c r e", e=2),
                ALU.mult,
            )
            nc.vector.quantize_mx(out=z2_codes[:, first:end].bitcast(FP8X4), scales=z2_scales[:, first:end], in_=woven)
        z_rest = tile([P, (TILES - 1) * W], BF16, "z_rest", last_d75)
        for t in range(1, TILES):
            z_q.append(z_columns(t, z_rest[:, (t - 1) * W : t * W]))

        out_rows = out.rearrange("(a t e) v -> t e a v", t=TILES, e=2)
        for t in range(TILES):
            last = t == TILES - 1
            half_s = tile([P, WIDE], F32, "half_s%d" % t)
            parts = Z2_PARTS if t == 0 else WHOLE
            for n, (first, end) in enumerate(parts):
                acc = product(z_q[t], 0, (z2_codes[:, first:end], z2_scales[:, first:end]), len(parts) - 1 - n)
                nc.scalar.activation(half_s[:, first:end], acc[:], ACT.Copy, scale=0.03125)
            s_n5 = tile([P, W], F32, "s_n5_%d" % t)
            st2 = tile([P, WIDE], F32, "st2_%d" % t)
            for first, end in HALVES if last else WHOLE:
                nc.scalar.activation(
                    s_n5[:, first:end], half_s[:].indirect(entries(list_n5, first, end)), ACT.Copy, scale=2.0
                )
                nc.vector.scalar_tensor_tensor(
                    st2[:, first:end], half_s[:, first:end], 2.0, s_n5[:, first:end], ALU.mult, ALU.max
                )
            result = tile([P, W], F32, "result%d" % t)
            if t < FIRST_SHARED_TILE:
                nc.vector.tensor_tensor(result[:], st2[:].indirect(list_n6[:]), half_s[:, :W], ALU.subtract)
                for e in range(2):
                    nc.sync.dma_start(out_rows[t, e], result[e:P:2, :])
            else:
                st2_n6 = tile([P, HALF], F32, "st2_n6_%d" % t)
                nc.scalar.activation(st2_n6[:], st2[:].indirect(entries(list_n6, HALF, W)), ACT.Copy)
                nc.vector.tensor_tensor(
                    result[:, :HALF], st2[:].indirect(entries(list_n6, 0, HALF)), half_s[:, :HALF], ALU.subtract
                )
                nc.vector.tensor_tensor(result[:, HALF:], st2_n6[:], half_s[:, HALF:W], ALU.subtract)
                for first, end in HALVES:
                    for e in range(2):
                        queue = nc.scalar if e and last else nc.sync
                        queue.dma_start(out_rows[t, e, :, first:end], result[e:P:2, first:end])
